import numpy as np
import ml_dtypes


def mxq(x, axis, fmt="e4m3"):
    dtype, down = {"e4m3": (ml_dtypes.float8_e4m3fn, 7), "e5m2": (ml_dtypes.float8_e5m2, 14)}[fmt]
    v = np.moveaxis(np.asarray(x, np.float32).astype(ml_dtypes.bfloat16).astype(np.float64), axis, -1)
    blocks = v.reshape(v.shape[:-1] + (-1, 32))
    amax = np.abs(blocks).max(-1, keepdims=True)
    byte = np.maximum(np.where(amax > 0, np.frexp(amax)[1] - 1 + 127, 0) - down, 1)
    scale = np.exp2(byte - 127.0)
    codes = (blocks / scale).astype(np.float32).astype(dtype).astype(np.float64)
    return np.moveaxis((codes * scale).reshape(v.shape), -1, axis)


WIDE = False


def mx_kscale(k):
    if not WIDE:
        return np.ones(k)
    levels = np.array([18, -18])
    if k % 512:
        return np.exp2(np.random.permutation(np.resize(levels, k // 32))).repeat(32)
    a = np.empty((k // 512, 16))
    for p in range(k // 512):
        a[p, :8] = np.random.permutation(np.resize(levels, 8))
        for g in range(8):
            far = levels[np.abs(levels - a[p, g]) >= 10]
            a[p, g + 8] = far[np.random.randint(len(far))]
    return np.exp2(a.ravel()).repeat(32)


def f64(x):
    return np.asarray(x).astype(np.float64)


def striped(idx):
    return np.tile(np.asarray(idx).reshape(-1, 16).T, (8, 1)).astype(np.uint16)


def unstriped(offs):
    return offs[:16].T.reshape(-1).astype(np.int64)


V, E, D, DV = 1024, 2048, 512, 512


def setup_inputs():
    n = np.random.standard_normal
    u = mx_kscale(E)
    coarse = lambda x: x.astype(np.float32).astype(ml_dtypes.bfloat16).astype(np.float64)
    return {
        "xT": (coarse(n((D, V)))).astype(np.float32),
        "dyT": (coarse(n((DV, V)))).astype(np.float32),
        "hE": coarse(n((DV, E))).astype(np.float32),
        "sw": np.tile(np.random.randint(8, 33, E) / 512.0 / u, (128, 1)).astype(np.float32),
        "tw": np.tile(np.random.randint(8, 33, E) / 16.0 * u, (128, 1)).astype(np.float32),
        "offs": striped(np.random.randint(0, V, E)),
        "offs2": striped(np.random.randint(0, V, E)),
    }


def reference(xT, dyT, hE, sw, tw, offs, offs2):
    h = f64(hE)
    xe = f64(sw)[:1] * f64(xT)[:, unstriped(offs)]
    dz = f64(tw)[:1] * f64(dyT)[:, unstriped(offs2)] * 2.0 * np.maximum(h, 0.0)
    return mxq(xe, 1, "e4m3") @ mxq(dz, 1, "e5m2").T

@@ -1,0 +1,242 @@
+from contextlib import ExitStack
+
+import concourse.mybir as mybir
+from concourse.masks import make_identity
+
+V, E, D, DV = 1024, 2048, 512, 512
+FLOPS = 2 * E * D * DV
+
+F32 = mybir.dt.float32
+BF16 = mybir.dt.bfloat16
+U32 = mybir.dt.uint32
+U16 = mybir.dt.uint16
+U8 = mybir.dt.uint8
+E4M3 = mybir.dt.float8_e4m3fn_x4
+E5M2 = mybir.dt.float8_e5m2_x4
+MULT = mybir.AluOpType.mult
+COPY = mybir.ActivationFunctionType.Copy
+RELU = mybir.ActivationFunctionType.Relu
+
+P = 128
+PACK = 4
+PASS = P * PACK
+PASSES = E // PASS
+BLOCKS = D // P
+COLS = PASS // 16
+PAIRS = 2 * PASSES
+RING = 2
+BANKS = 4
+SLABS = 3
+Z_ORDER = [0, 2, 1, 3, 4, 5, 6, 7]
+AHEAD = 4
+FIRST_MIXED = 2
+VECTOR_PAIRS = (7,)
+
+
+def tile_attend_gmw_kernel(tc, xT, dyT, hE, sw, tw, offs, offs2, out):
+    nc = tc.nc
+    with ExitStack() as ctx:
+        held = ctx.enter_context(tc.tile_pool(name="held", bufs=1))
+        work = ctx.enter_context(tc.tile_pool(name="work", bufs=3))
+        psum = ctx.enter_context(tc.psum_pool(name="psum", bufs=1))
+
+        src = held.tile([P, E // 16], U16, name="src")
+        dst = held.tile([P, E // 16], U16, name="dst")
+        xw = [held.tile([P, V], F32, name="xw%d" % b) for b in range(BLOCKS)]
+        dyw = [held.tile([P, V], F32, name="dyw%d" % b) for b in range(BLOCKS)]
+        sws = [held.tile([P, PASS], F32, name="sw%d" % g) for g in range(PASSES)]
+        hs = [held.tile([P, 2 * PASS], F32, name="h%d" % q, align_bytes=64) for q in range(PAIRS)]
+        slabs = [held.tile([P, 2 * PASS], F32, name="slab%d" % k) for k in range(SLABS)]
+        twc = held.tile([P, PASSES * PACK], F32, name="twc")
+        ident = held.tile([P, P], F32, name="ident")
+        make_identity(nc, ident[:])
+
+        def load_sw(g):
+            nc.sync.dma_start(out=sws[g][:], in_=sw[:, g * PASS:(g + 1) * PASS])
+
+        def load_h(q):
+            g, j = divmod(q, 2)
+            nc.sync.dma_start(out=hs[q][:].rearrange("p (b e) -> p b e", b=2), in_=hE[2 * j * P:2 * (j + 1) * P, g * PASS:(g + 1) * PASS].rearrange("(b p) e -> p b e", p=P))
+
+        def load_small():
+            nc.sync.dma_start(dst[:], offs2)
+            nc.sync.dma_start(out=twc[:].rearrange("p (g t) -> p g t", t=PACK),
+                              in_=tw[0, :].rearrange("(g p t) -> p g t", p=P, t=PACK))
+
+        def load_table(tiles, table, b):
+            nc.sync.dma_start(out=tiles[b][:], in_=table[b * P:(b + 1) * P, :])
+
+        nc.sync.dma_start(src[:], offs)
+        load_table(xw, xT, 0)
+        load_sw(0)
+        load_sw(1)
+        load_sw(2)
+        load_h(0)
+        load_small()
+        load_table(dyw, dyT, 0)
+        load_table(dyw, dyT, 1)
+        load_h(2)
+        load_table(xw, xT, 1)
+        load_h(1)
+        load_table(dyw, dyT, 2)
+        load_table(dyw, dyT, 3)
+        load_table(xw, xT, 2)
+        load_h(3)
+        load_table(xw, xT, 3)
+        load_h(4)
+        load_h(5)
+        load_h(6)
+        load_sw(3)
+        load_h(7)
+
+        x_words = [[held.tile([P, P], U32, name="xq%d_%d" % (b, g), align_bytes=64) for g in range(PASSES)] for b in range(BLOCKS)]
+        x_scales = [[held.tile([P, P], U8, name="xs%d_%d" % (b, g), align_bytes=64) for g in range(PASSES)] for b in range(BLOCKS)]
+        x_in = [[held.tile([P, PASS], BF16, name="xi%d_%d" % (b, g), align_bytes=64)[:] for g in range(PASSES)] for b in range(BLOCKS)]
+        z_words = [held.tile([P, DV], U32, name="zq%d" % g, align_bytes=64) for g in range(PASSES)]
+        z_scales = [held.tile([P, DV], U8, name="zs%d" % g, align_bytes=64) for g in range(PASSES)]
+        z_in = [held.tile([P, DV * PACK], BF16, name="zi%d" % g, align_bytes=64) for g in range(PASSES)]
+        acc = [psum.tile([P, DV], F32, name="acc%d" % b) for b in range(BLOCKS)]
+        banks = [psum.tile([P, PASS], F32, name="bank%d" % k) for k in range(BANKS)]
+        prods = [held.tile([P, PASS], F32, name="prod%d" % k, align_bytes=64) for k in range(RING)]
+        used = {"bank": 0, "prod": 0}
+
+        def take(ring, kind):
+            used[kind] = used[kind] + 1
+            return ring[(used[kind] - 1) % len(ring)][:]
+
+        def gather(window, lst, g, factor, prod=None):
+            if prod is None:
+                prod = take(prods, "prod")
+            nc.vector.tensor_tensor(prod, window[:].indirect(lst[:, g * COLS:(g + 1) * COLS]), factor, MULT)
+            return prod
+
+        def turn_f32(prod):
+            bank = take(banks, "bank").rearrange("p (t d) -> p t d", t=PACK)
+            for t in range(PACK):
+                nc.tensor.transpose(bank[:, t, :], prod[:, t:PASS:PACK], ident[:])
+            return bank
+
+        def x_quantise(b, g):
+            nc.vector.quantize_mx(out=x_words[b][g][:].bitcast(E4M3), scales=x_scales[b][g][:], in_=x_in[b][g])
+
+        def x_turn(b, g, prod, paired):
+            if not paired:
+                return turn_f32(prod)
+            pairs = work.tile([P, PASS], BF16, name="pairs")
+            nc.scalar.copy(out=pairs[:].rearrange("p (u s e) -> p u s e", u=2, e=2),
+                           in_=prod.rearrange("p (s u e) -> p u s e", u=2, e=2))
+            bank = take(banks, "bank").rearrange("p (t d) -> p t d", t=PACK)
+            words = pairs[:].bitcast(F32)
+            for u in range(2):
+                nc.tensor.transpose(bank[:, u, :], words[:, u * P:(u + 1) * P], ident[:])
+            return bank
+
+        def x_out(b, g, bank, paired):
+            if paired:
+                nc.scalar.copy(out=x_in[b][g].bitcast(F32).rearrange("p (d u) -> p d u", u=2),
+                               in_=bank[:, 0:2, :].rearrange("p u d -> p d u"))
+            else:
+                nc.scalar.copy(out=x_in[b][g].rearrange("p (d t) -> p d t", t=PACK), in_=bank.rearrange("p t d -> p d t"))
+            x_quantise(b, g)
+            done["x"].append((b, g))
+            products()
+
+        def relu(r):
+            nc.scalar.activation(out=slabs[r % SLABS][:], in_=hs[Z_ORDER[r]][:], func=RELU, scale=2.0)
+
+        def plane_view(r):
+            return slabs[r % SLABS][:].bitcast(BF16).rearrange("p (h t n) -> p h t n", h=2, n=2 * P)[:, :, 0:2, :]
+
+        def z_scalar(r):
+            g, j = divmod(Z_ORDER[r], 2)
+            pr = [gather(dyw[2 * j + i], dst, g, slabs[r % SLABS][:, i * PASS:(i + 1) * PASS]) for i in range(2)]
+            two = [take(banks, "bank").rearrange("p (t n) -> p t n", t=2) for h in range(2)]
+            for i in range(2):
+                for t in range(PACK):
+                    nc.tensor.transpose(two[t // 2][:, t % 2, i * P:(i + 1) * P], pr[i][:, t:PASS:PACK], ident[:])
+            planes = plane_view(r)
+            for t in range(PACK):
+                nc.scalar.activation(out=planes[:, t // 2, t % 2, :], in_=two[t // 2][:, t % 2, :], func=COPY,
+                                     scale=twc[:, g * PACK + t:g * PACK + t + 1])
+
+        def z_weave(r):
+            g, j = divmod(Z_ORDER[r], 2)
+            nc.scalar.copy(out=z_in[g][:, j * 2 * PASS:(j + 1) * 2 * PASS].rearrange("p (c i h t) -> p c h t i", i=4, h=2, t=2),
+                           in_=plane_view(r).rearrange("p h t (c i) -> p c h t i", i=4))
+
+        def z_vector(r):
+            g, j = divmod(Z_ORDER[r], 2)
+            for i in range(2):
+                b = 2 * j + i
+                bank = turn_f32(gather(dyw[b], dst, g, slabs[r % SLABS][:, i * PASS:(i + 1) * PASS]))
+                nc.vector.tensor_tensor(z_in[g][:, b * PASS:(b + 1) * PASS].rearrange("p (n t) -> p n t", t=PACK),
+                                        bank.rearrange("p t n -> p n t"),
+                                        twc[:, g * PACK:(g + 1) * PACK].unsqueeze(1).to_broadcast([P, P, PACK]), MULT)
+
+        def z_quantise(g):
+            nc.vector.quantize_mx(out=z_words[g][:].bitcast(E5M2), scales=z_scales[g][:], in_=z_in[g][:])
+
+        def multiply(b, g):
+            nc.tensor.matmul_mx(out=acc[b][:], lhsT=x_words[b][g][:].bitcast(E4M3), lhsT_scale=x_scales[b][g][:],
+                                rhs=z_words[g][:].bitcast(E5M2), rhs_scale=z_scales[g][:],
+                                start=(g == 0), stop=(g == PASSES - 1))
+
+        x_order = [(0, 0), (0, 1), (0, 2), (1, 0), (1, 1), (2, 0), (3, 0), (2, 1), (3, 1), (1, 2), (2, 2), (3, 2)] + [(b, 3) for b in range(BLOCKS)]
+        counts = [3,0,2,2,2,2,2,1,2]
+        done = {"x": [], "z": [], "m": [], "r": []}
+
+        def products():
+            for g in range(PASSES):
+                for b in range(BLOCKS):
+                    if (b, g) in done["x"] and g in done["z"] and (b, g) not in done["m"] and (g == 0 or (b, g - 1) in done["m"]):
+                        multiply(b, g)
+                        done["m"].append((b, g))
+                        if g == PASSES - 1:
+                            result = work.tile([P, DV], F32, name="result")
+                            if b % 2 == 1:
+                                nc.vector.tensor_copy(out=result[:], in_=acc[b][:])
+                            else:
+                                nc.scalar.copy(out=result[:], in_=acc[b][:])
+                            nc.sync.dma_start(out=out[b * P:(b + 1) * P, :], in_=result[:])
+
+        def x_gather(i, prod):
+            b, g = x_order[i]
+            return (b, g, gather(xw[b], src, g, sws[g][:], prod), i in (4, 6, 8, 10, 12, 14, 15,))
+
+        def finish_z(r):
+            if r not in VECTOR_PAIRS:
+                z_weave(r)
+            done["r"].append(Z_ORDER[r])
+            g = Z_ORDER[r] // 2
+            if 2 * g in done["r"] and 2 * g + 1 in done["r"]:
+                z_quantise(g)
+                done["z"].append(g)
+                products()
+
+        for k in range(counts[0]):
+            x_in[0][k] = hs[Z_ORDER[0]][:].bitcast(BF16)[:, k * PASS:(k + 1) * PASS]
+        relu(0)
+        relu(1)
+        i = 0
+        for k in range(counts[0]):
+            u = x_gather(i, slabs[2][:, (k - 2) * PASS:(k - 1) * PASS] if k >= 2 else None)
+            x_out(u[0], u[1], x_turn(*u), u[3])
+            i = i + 1
+        for r in range(PAIRS):
+            if r in VECTOR_PAIRS:
+                z_vector(r)
+            else:
+                z_scalar(r)
+            slots = [slabs[(r - 1) % SLABS][:, k * PASS:(k + 1) * PASS] if r > 0 and k < 2 else None for k in range(counts[r + 1])]
+            if r == PAIRS - 1:
+                slots = [hs[Z_ORDER[r]][:, k * PASS:(k + 1) * PASS] for k in range(2)]
+            units = [x_gather(i + k, s) for k, s in enumerate(slots)]
+            i = i + len(units)
+            banks_of = [x_turn(*u) for u in units]
+            finish_z(r)
+            for k, u in enumerate(units):
+                if k == 1 and r + 2 < PAIRS:
+                    relu(r + 2)
+                x_out(u[0], u[1], banks_of[k], u[3])
+            if len(units) < 2 and r + 2 < PAIRS:
+                relu(r + 2)

@@ -23,40 +23,42 @@ PASS = P * PACK
 PASSES = E // PASS
 BLOCKS = D // P
 COLS = PASS // 16
-PAIRS = 2 * PASSES
-RING = 2
+ROUNDS = 2 * PASSES
+LAST = ROUNDS - 1
 BANKS = 4
+HEAD = 4
 SLABS = 3
-Z_ORDER = [0, 2, 1, 3, 4, 5, 6, 7]
-AHEAD = 4
-FIRST_MIXED = 2
-VECTOR_PAIRS = (7,)
+PAD = 32
+Z_ORDER = [(0, 0), (1, 0), (0, 1), (1, 1), (2, 0), (2, 1), (3, 0), (3, 1)]
 
 
 def tile_attend_gmw_kernel(tc, xT, dyT, hE, sw, tw, offs, offs2, out):
     nc = tc.nc
     with ExitStack() as ctx:
         held = ctx.enter_context(tc.tile_pool(name="held", bufs=1))
-        work = ctx.enter_context(tc.tile_pool(name="work", bufs=3))
         psum = ctx.enter_context(tc.psum_pool(name="psum", bufs=1))
 
         src = held.tile([P, E // 16], U16, name="src")
         dst = held.tile([P, E // 16], U16, name="dst")
-        xw = [held.tile([P, V], F32, name="xw%d" % b) for b in range(BLOCKS)]
+        xw = [held.tile([P, V + PAD], F32, name="xw%d" % b) for b in range(BLOCKS)]
         dyw = [held.tile([P, V], F32, name="dyw%d" % b) for b in range(BLOCKS)]
-        sws = [held.tile([P, PASS], F32, name="sw%d" % g) for g in range(PASSES)]
-        hs = [held.tile([P, 2 * PASS], F32, name="h%d" % q, align_bytes=64) for q in range(PAIRS)]
+        sws = held.tile([P, E], F32, name="sws")
+        hs = [held.tile([P, 2 * PASS], F32, name="h%d" % r, align_bytes=64) for r in range(ROUNDS)]
         slabs = [held.tile([P, 2 * PASS], F32, name="slab%d" % k) for k in range(SLABS)]
         twc = held.tile([P, PASSES * PACK], F32, name="twc")
         ident = held.tile([P, P], F32, name="ident")
         make_identity(nc, ident[:])
+        for b in range(1, BLOCKS):
+            nc.gpsimd.memset(xw[b][:, V:V + PAD], 0.0)
+        nc.gpsimd.memset(xw[0][:, V:V + PAD], 0.0)
 
         def load_sw(g):
-            nc.sync.dma_start(out=sws[g][:], in_=sw[:, g * PASS:(g + 1) * PASS])
+            nc.sync.dma_start(out=sws[:, g * PASS:(g + 1) * PASS], in_=sw[:, g * PASS:(g + 1) * PASS])
 
-        def load_h(q):
-            g, j = divmod(q, 2)
-            nc.sync.dma_start(out=hs[q][:].rearrange("p (b e) -> p b e", b=2), in_=hE[2 * j * P:2 * (j + 1) * P, g * PASS:(g + 1) * PASS].rearrange("(b p) e -> p b e", p=P))
+        def load_h(r):
+            g, j = Z_ORDER[r]
+            nc.sync.dma_start(out=hs[r][:].rearrange("p (i e) -> p i e", i=2),
+                              in_=hE[2 * j * P:2 * (j + 1) * P, g * PASS:(g + 1) * PASS].rearrange("(i p) e -> p i e", p=P))
 
         def load_small():
             nc.sync.dma_start(dst[:], offs2)
@@ -64,20 +66,21 @@ def tile_attend_gmw_kernel(tc, xT, dyT, hE, sw, tw, offs, offs2, out):
                               in_=tw[0, :].rearrange("(g p t) -> p g t", p=P, t=PACK))
 
         def load_table(tiles, table, b):
-            nc.sync.dma_start(out=tiles[b][:], in_=table[b * P:(b + 1) * P, :])
+            nc.sync.dma_start(out=tiles[b][:, 0:V], in_=table[b * P:(b + 1) * P, :])
 
         nc.sync.dma_start(src[:], offs)
         load_table(xw, xT, 0)
         load_sw(0)
         load_sw(1)
-        load_sw(2)
         load_h(0)
+        load_sw(2)
+        load_sw(3)
         load_small()
+        load_h(1)
         load_table(dyw, dyT, 0)
         load_table(dyw, dyT, 1)
-        load_h(2)
         load_table(xw, xT, 1)
-        load_h(1)
+        load_h(2)
         load_table(dyw, dyT, 2)
         load_table(dyw, dyT, 3)
         load_table(xw, xT, 2)
@@ -86,157 +89,186 @@ def tile_attend_gmw_kernel(tc, xT, dyT, hE, sw, tw, offs, offs2, out):
         load_h(4)
         load_h(5)
         load_h(6)
-        load_sw(3)
         load_h(7)
 
-        x_words = [[held.tile([P, P], U32, name="xq%d_%d" % (b, g), align_bytes=64) for g in range(PASSES)] for b in range(BLOCKS)]
-        x_scales = [[held.tile([P, P], U8, name="xs%d_%d" % (b, g), align_bytes=64) for g in range(PASSES)] for b in range(BLOCKS)]
-        x_in = [[held.tile([P, PASS], BF16, name="xi%d_%d" % (b, g), align_bytes=64)[:] for g in range(PASSES)] for b in range(BLOCKS)]
-        z_words = [held.tile([P, DV], U32, name="zq%d" % g, align_bytes=64) for g in range(PASSES)]
+        x_words = [held.tile([P, PASSES * P], U32, name="xq%d" % b, align_bytes=64) for b in range(BLOCKS)]
+        x_scales = [held.tile([P, PASSES * P], U8, name="xs%d" % b, align_bytes=64) for b in range(BLOCKS)]
+        x_in = [[held.tile([P, 2 * PASS], BF16, name="xi%d_%d" % (b, h), align_bytes=64)[:] for h in range(2)] for b in range(BLOCKS)]
+        x_in[0] = [hs[h][:, 0:PASS].bitcast(BF16) for h in range(2)]
+        spare = held.tile([P, 2 * PASS], F32, name="spare")
+        z_words = [held.tile([P, DV], U32, name="zq%d" % g, align_bytes=64)[:] for g in range(PASSES)]
         z_scales = [held.tile([P, DV], U8, name="zs%d" % g, align_bytes=64) for g in range(PASSES)]
         z_in = [held.tile([P, DV * PACK], BF16, name="zi%d" % g, align_bytes=64) for g in range(PASSES)]
         acc = [psum.tile([P, DV], F32, name="acc%d" % b) for b in range(BLOCKS)]
         banks = [psum.tile([P, PASS], F32, name="bank%d" % k) for k in range(BANKS)]
-        prods = [held.tile([P, PASS], F32, name="prod%d" % k, align_bytes=64) for k in range(RING)]
-        used = {"bank": 0, "prod": 0}
+        z_prod = [held.tile([P, PASS], F32, name="prod%d" % i, align_bytes=64) for i in range(2)]
+        pairs = [held.tile([P, PASS], BF16, name="pairs%d" % i) for i in range(2)]
+        results = [held.tile([P, DV], F32, name="result%d" % b) for b in range(BLOCKS)]
+        turns = []
+        x_ready, z_ready, multiplied = [], [], []
 
-        def take(ring, kind):
-            used[kind] = used[kind] + 1
-            return ring[(used[kind] - 1) % len(ring)][:]
+        def next_bank():
+            turns.append(banks[len(turns) % BANKS])
+            return turns[-1][:]
 
-        def gather(window, lst, g, factor, prod=None):
-            if prod is None:
-                prod = take(prods, "prod")
-            nc.vector.tensor_tensor(prod, window[:].indirect(lst[:, g * COLS:(g + 1) * COLS]), factor, MULT)
-            return prod
+        def gather(prod, window, lst, g, passes, factor):
+            nc.vector.tensor_tensor(prod, window[:].indirect(lst[:, g * COLS:(g + passes) * COLS]), factor, MULT)
 
-        def turn_f32(prod):
-            bank = take(banks, "bank").rearrange("p (t d) -> p t d", t=PACK)
+        def x_gather(prod, b, g, passes):
+            gather(prod, xw[b], src, g, passes, sws[:, g * PASS:(g + passes) * PASS])
+
+        def turn_floats(prod):
+            bank = next_bank().rearrange("p (t d) -> p t d", t=PACK)
             for t in range(PACK):
                 nc.tensor.transpose(bank[:, t, :], prod[:, t:PASS:PACK], ident[:])
             return bank
 
-        def x_quantise(b, g):
-            nc.vector.quantize_mx(out=x_words[b][g][:].bitcast(E4M3), scales=x_scales[b][g][:], in_=x_in[b][g])
-
-        def x_turn(b, g, prod, paired):
-            if not paired:
-                return turn_f32(prod)
-            pairs = work.tile([P, PASS], BF16, name="pairs")
-            nc.scalar.copy(out=pairs[:].rearrange("p (u s e) -> p u s e", u=2, e=2),
+        def turn_pairs(prod, rounded):
+            nc.scalar.copy(out=rounded[:].rearrange("p (u s e) -> p u s e", u=2, e=2),
                            in_=prod.rearrange("p (s u e) -> p u s e", u=2, e=2))
-            bank = take(banks, "bank").rearrange("p (t d) -> p t d", t=PACK)
-            words = pairs[:].bitcast(F32)
+            bank = next_bank().rearrange("p (t d) -> p t d", t=PACK)
+            words = rounded[:].bitcast(F32)
             for u in range(2):
                 nc.tensor.transpose(bank[:, u, :], words[:, u * P:(u + 1) * P], ident[:])
             return bank
 
-        def x_out(b, g, bank, paired):
-            if paired:
-                nc.scalar.copy(out=x_in[b][g].bitcast(F32).rearrange("p (d u) -> p d u", u=2),
-                               in_=bank[:, 0:2, :].rearrange("p u d -> p d u"))
-            else:
-                nc.scalar.copy(out=x_in[b][g].rearrange("p (d t) -> p d t", t=PACK), in_=bank.rearrange("p t d -> p d t"))
-            x_quantise(b, g)
-            done["x"].append((b, g))
-            products()
+        def floats_out(b, g, bank):
+            nc.scalar.copy(out=x_in[b][g // 2][:, g % 2 * PASS:(g % 2 + 1) * PASS].rearrange("p (d t) -> p d t", t=PACK),
+                           in_=bank.rearrange("p t d -> p d t"))
+
+        def pairs_out(b, g, bank):
+            nc.scalar.copy(out=x_in[b][g // 2][:, g % 2 * PASS:(g % 2 + 1) * PASS].bitcast(F32).rearrange("p (d u) -> p d u", u=2),
+                           in_=bank[:, 0:2, :].rearrange("p u d -> p d u"))
+
+        def x_quantise(b, g, passes):
+            cols = slice(g * P, (g + passes) * P)
+            nc.vector.quantize_mx(out=x_words[b][:, cols].bitcast(E4M3), scales=x_scales[b][:, cols],
+                                  in_=x_in[b][g // 2][:, g % 2 * PASS:(g % 2 + passes) * PASS])
+            x_ready.extend((b, g + k) for k in range(passes))
+            multiply_ready()
 
         def relu(r):
-            nc.scalar.activation(out=slabs[r % SLABS][:], in_=hs[Z_ORDER[r]][:], func=RELU, scale=2.0)
+            nc.scalar.activation(out=slabs[r % SLABS][:], in_=hs[r][:], func=RELU, scale=2.0)
 
-        def plane_view(r):
+        def z_gather(r, i):
+            g, j = Z_ORDER[r]
+            gather(z_prod[i][:], dyw[2 * j + i], dst, g, 1, slabs[r % SLABS][:, i * PASS:(i + 1) * PASS])
+
+        def tw_column(g, t):
+            return twc[:, g * PACK + t:g * PACK + t + 1]
+
+        def planes(r):
             return slabs[r % SLABS][:].bitcast(BF16).rearrange("p (h t n) -> p h t n", h=2, n=2 * P)[:, :, 0:2, :]
 
-        def z_scalar(r):
-            g, j = divmod(Z_ORDER[r], 2)
-            pr = [gather(dyw[2 * j + i], dst, g, slabs[r % SLABS][:, i * PASS:(i + 1) * PASS]) for i in range(2)]
-            two = [take(banks, "bank").rearrange("p (t n) -> p t n", t=2) for h in range(2)]
+        def z_turn_and_scale(r):
+            g, j = Z_ORDER[r]
+            two = [next_bank().rearrange("p (t n) -> p t n", t=2) for h in range(2)]
             for i in range(2):
                 for t in range(PACK):
-                    nc.tensor.transpose(two[t // 2][:, t % 2, i * P:(i + 1) * P], pr[i][:, t:PASS:PACK], ident[:])
-            planes = plane_view(r)
+                    nc.tensor.transpose(two[t // 2][:, t % 2, i * P:(i + 1) * P], z_prod[i][:, t:PASS:PACK], ident[:])
             for t in range(PACK):
-                nc.scalar.activation(out=planes[:, t // 2, t % 2, :], in_=two[t // 2][:, t % 2, :], func=COPY,
-                                     scale=twc[:, g * PACK + t:g * PACK + t + 1])
+                nc.scalar.activation(out=planes(r)[:, t // 2, t % 2, :], in_=two[t // 2][:, t % 2, :], func=COPY,
+                                     scale=tw_column(g, t))
 
         def z_weave(r):
-            g, j = divmod(Z_ORDER[r], 2)
+            g, j = Z_ORDER[r]
             nc.scalar.copy(out=z_in[g][:, j * 2 * PASS:(j + 1) * 2 * PASS].rearrange("p (c i h t) -> p c h t i", i=4, h=2, t=2),
-                           in_=plane_view(r).rearrange("p h t (c i) -> p c h t i", i=4))
+                           in_=planes(r).rearrange("p h t (c i) -> p c h t i", i=4))
 
-        def z_vector(r):
-            g, j = divmod(Z_ORDER[r], 2)
-            for i in range(2):
-                b = 2 * j + i
-                bank = turn_f32(gather(dyw[b], dst, g, slabs[r % SLABS][:, i * PASS:(i + 1) * PASS]))
-                nc.vector.tensor_tensor(z_in[g][:, b * PASS:(b + 1) * PASS].rearrange("p (n t) -> p n t", t=PACK),
-                                        bank.rearrange("p t n -> p n t"),
-                                        twc[:, g * PACK:(g + 1) * PACK].unsqueeze(1).to_broadcast([P, P, PACK]), MULT)
+        def z_block_on_scalar(r, i):
+            g, j = Z_ORDER[r]
+            bank = turn_floats(z_prod[i][:])
+            flat = slabs[r % SLABS][:, i * PASS:(i + 1) * PASS].bitcast(BF16)[:, 0:PASS].rearrange("p (t n) -> p t n", t=PACK)
+            for t in range(PACK):
+                nc.scalar.activation(out=flat[:, t, :], in_=bank[:, t, :], func=COPY, scale=tw_column(g, t))
+            b = 2 * j + i
+            nc.scalar.copy(out=z_in[g][:, b * PASS:(b + 1) * PASS].rearrange("p (c i t) -> p c t i", i=4, t=PACK),
+                           in_=flat.rearrange("p t (c i) -> p c t i", i=4))
+
+        def z_block_on_vector(r, i):
+            g, j = Z_ORDER[r]
+            b = 2 * j + i
+            bank = turn_floats(z_prod[i][:])
+            nc.vector.tensor_tensor(z_in[g][:, b * PASS:(b + 1) * PASS].rearrange("p (n t) -> p n t", t=PACK),
+                                    bank.rearrange("p t n -> p n t"),
+                                    twc[:, g * PACK:(g + 1) * PACK].unsqueeze(1).to_broadcast([P, P, PACK]), MULT)
 
         def z_quantise(g):
-            nc.vector.quantize_mx(out=z_words[g][:].bitcast(E5M2), scales=z_scales[g][:], in_=z_in[g][:])
+            nc.vector.quantize_mx(out=z_words[g].bitcast(E5M2), scales=z_scales[g][:], in_=z_in[g][:])
+            z_ready.append(g)
+            multiply_ready()
 
-        def multiply(b, g):
-            nc.tensor.matmul_mx(out=acc[b][:], lhsT=x_words[b][g][:].bitcast(E4M3), lhsT_scale=x_scales[b][g][:],
-                                rhs=z_words[g][:].bitcast(E5M2), rhs_scale=z_scales[g][:],
-                                start=(g == 0), stop=(g == PASSES - 1))
-
-        x_order = [(0, 0), (0, 1), (0, 2), (1, 0), (1, 1), (2, 0), (3, 0), (2, 1), (3, 1), (1, 2), (2, 2), (3, 2)] + [(b, 3) for b in range(BLOCKS)]
-        counts = [3,0,2,2,2,2,2,1,2]
-        done = {"x": [], "z": [], "m": [], "r": []}
-
-        def products():
-            for g in range(PASSES):
+        def multiply_ready():
+            for g in z_ready:
                 for b in range(BLOCKS):
-                    if (b, g) in done["x"] and g in done["z"] and (b, g) not in done["m"] and (g == 0 or (b, g - 1) in done["m"]):
-                        multiply(b, g)
-                        done["m"].append((b, g))
-                        if g == PASSES - 1:
-                            result = work.tile([P, DV], F32, name="result")
-                            if b % 2 == 1:
-                                nc.vector.tensor_copy(out=result[:], in_=acc[b][:])
-                            else:
-                                nc.scalar.copy(out=result[:], in_=acc[b][:])
-                            nc.sync.dma_start(out=out[b * P:(b + 1) * P, :], in_=result[:])
+                    if (b, g) in x_ready and (b, g) not in multiplied:
+                        cols = slice(g * P, (g + 1) * P)
+                        nc.tensor.matmul_mx(out=acc[b][:], lhsT=x_words[b][:, cols].bitcast(E4M3), lhsT_scale=x_scales[b][:, cols],
+                                            rhs=z_words[g].bitcast(E5M2), rhs_scale=z_scales[g][:],
+                                            start=(g == 0), stop=(g == PASSES - 1))
+                        multiplied.append((b, g))
 
-        def x_gather(i, prod):
-            b, g = x_order[i]
-            return (b, g, gather(xw[b], src, g, sws[g][:], prod), i in (4, 6, 8, 10, 12, 14, 15,))
-
-        def finish_z(r):
-            if r not in VECTOR_PAIRS:
-                z_weave(r)
-            done["r"].append(Z_ORDER[r])
-            g = Z_ORDER[r] // 2
-            if 2 * g in done["r"] and 2 * g + 1 in done["r"]:
-                z_quantise(g)
-                done["z"].append(g)
-                products()
-
-        for k in range(counts[0]):
-            x_in[0][k] = hs[Z_ORDER[0]][:].bitcast(BF16)[:, k * PASS:(k + 1) * PASS]
         relu(0)
         relu(1)
-        i = 0
-        for k in range(counts[0]):
-            u = x_gather(i, slabs[2][:, (k - 2) * PASS:(k - 1) * PASS] if k >= 2 else None)
-            x_out(u[0], u[1], x_turn(*u), u[3])
-            i = i + 1
-        for r in range(PAIRS):
-            if r in VECTOR_PAIRS:
-                z_vector(r)
+        head = [z_prod[0][:], z_prod[1][:], slabs[2][:, 0:PASS], slabs[2][:, PASS:2 * PASS]]
+        for g in range(HEAD):
+            x_gather(head[g], 0, g, 1)
+            floats_out(0, g, turn_floats(head[g]))
+            x_quantise(0, g, 1)
+        x_left = [(1, 0), (1, 1), (2, 0), (2, 1), (3, 0), (3, 1), (1, 2), (1, 3), (2, 2), (3, 2), (2, 3), (3, 3)]
+        counts = [0, 2, 2, 2, 2, 2, 0]
+        late = None
+
+        def finish_late(unit):
+            pairs_out(*unit)
+            x_quantise(unit[0], unit[1], 1)
+
+        for r in range(LAST):
+            z_gather(r, 0)
+            z_gather(r, 1)
+            z_turn_and_scale(r)
+            if late is not None:
+                finish_late(late)
+                late = None
+            units = x_left[sum(counts[:r]):sum(counts[:r + 1])]
+            slab = slabs[(r - 1) % SLABS] if r > 1 else spare
+            if PAD and len(units) == 2 and units[1] == (units[0][0], units[0][1] + 1):
+                x_gather(slab[:], units[0][0], units[0][1], 2)
             else:
-                z_scalar(r)
-            slots = [slabs[(r - 1) % SLABS][:, k * PASS:(k + 1) * PASS] if r > 0 and k < 2 else None for k in range(counts[r + 1])]
-            if r == PAIRS - 1:
-                slots = [hs[Z_ORDER[r]][:, k * PASS:(k + 1) * PASS] for k in range(2)]
-            units = [x_gather(i + k, s) for k, s in enumerate(slots)]
-            i = i + len(units)
-            banks_of = [x_turn(*u) for u in units]
-            finish_z(r)
-            for k, u in enumerate(units):
-                if k == 1 and r + 2 < PAIRS:
-                    relu(r + 2)
-                x_out(u[0], u[1], banks_of[k], u[3])
-            if len(units) < 2 and r + 2 < PAIRS:
+                for k, (b, g) in enumerate(units):
+                    x_gather(slab[:, k * PASS:(k + 1) * PASS], b, g, 1)
+            now = None
+            if len(units) == 2:
+                now = units[0] + (turn_floats(slab[:, 0:PASS]),)
+            if units:
+                late = units[-1] + (turn_pairs(slab[:, (len(units) - 1) * PASS:len(units) * PASS], pairs[r % 2]),)
+            if True and r + 2 == LAST:
+                relu(LAST)
+            z_weave(r)
+            g, j = Z_ORDER[r]
+            if j == 1:
+                z_quantise(g)
+            if now is not None:
+                floats_out(*now)
+                x_quantise(now[0], now[1], 1)
+            if r + 2 < ROUNDS and not (True and r + 2 == LAST):
                 relu(r + 2)
+        if late is not None:
+            finish_late(late)
+        z_gather(LAST, 0)
+        z_gather(LAST, 1)
+        units = x_left[-2:]
+        for k, (b, g) in enumerate(units):
+            x_gather(hs[LAST][:, k * PASS:(k + 1) * PASS], b, g, 1)
+        z_block_on_scalar(LAST, 0)
+        z_block_on_vector(LAST, 1)
+        last = [turn_pairs(hs[LAST][:, k * PASS:(k + 1) * PASS], pairs[k]) for k in range(2)]
+        z_quantise(PASSES - 1)
+        for k in range(2):
+            finish_late(units[k] + (last[k],))
+        for b in range(BLOCKS):
+            if b % 2 == 1:
+                nc.vector.tensor_copy(out=results[b][:], in_=acc[b][:])
+            else:
+                nc.scalar.copy(out=results[b][:], in_=acc[b][:])
+            nc.sync.dma_start(out=out[b * P:(b + 1) * P, :], in_=results[b][:])

@@ -26,7 +26,7 @@ COLS = PASS // 16
 ROUNDS = 2 * PASSES
 LAST = ROUNDS - 1
 BANKS = 4
-HEAD = 4
+HEAD = 3
 SLABS = 3
 PAD = 32
 Z_ORDER = [(0, 0), (1, 0), (0, 1), (1, 1), (2, 0), (2, 1), (3, 0), (3, 1)]
@@ -61,32 +61,32 @@ def tile_attend_gmw_kernel(tc, xT, dyT, hE, sw, tw, offs, offs2, out):
                               in_=hE[2 * j * P:2 * (j + 1) * P, g * PASS:(g + 1) * PASS].rearrange("(i p) e -> p i e", p=P))
 
         def load_small():
-            nc.sync.dma_start(dst[:], offs2)
             nc.sync.dma_start(out=twc[:].rearrange("p (g t) -> p g t", t=PACK),
                               in_=tw[0, :].rearrange("(g p t) -> p g t", p=P, t=PACK))
 
         def load_table(tiles, table, b):
             nc.sync.dma_start(out=tiles[b][:, 0:V], in_=table[b * P:(b + 1) * P, :])
 
-        nc.sync.dma_start(src[:], offs)
         load_table(xw, xT, 0)
+        nc.sync.dma_start(src[:], offs)
         load_sw(0)
         load_sw(1)
         load_h(0)
         load_sw(2)
-        load_sw(3)
-        load_small()
         load_h(1)
+        nc.sync.dma_start(dst[:], offs2)
         load_table(dyw, dyT, 0)
         load_table(dyw, dyT, 1)
-        load_table(xw, xT, 1)
+        load_small()
         load_h(2)
+        load_table(xw, xT, 1)
         load_table(dyw, dyT, 2)
         load_table(dyw, dyT, 3)
         load_table(xw, xT, 2)
         load_h(3)
         load_table(xw, xT, 3)
         load_h(4)
+        load_sw(3)
         load_h(5)
         load_h(6)
         load_h(7)
@@ -102,8 +102,11 @@ def tile_attend_gmw_kernel(tc, xT, dyT, hE, sw, tw, offs, offs2, out):
         acc = [psum.tile([P, DV], F32, name="acc%d" % b) for b in range(BLOCKS)]
         banks = [psum.tile([P, PASS], F32, name="bank%d" % k) for k in range(BANKS)]
         z_prod = [held.tile([P, PASS], F32, name="prod%d" % i, align_bytes=64) for i in range(2)]
-        pairs = [held.tile([P, PASS], BF16, name="pairs%d" % i) for i in range(2)]
-        results = [held.tile([P, DV], F32, name="result%d" % b) for b in range(BLOCKS)]
+        pair_bufs = [held.tile([P, PASS], F32, name="pairs%d" % i) for i in range(2)]
+        pairs = [buf[:].bitcast(BF16)[:, 0:PASS] for buf in pair_bufs]
+        results = [held.tile([P, DV], F32, name="result%d" % b)[:] for b in range(BLOCKS)]
+        results[0] = pair_bufs[1][:]
+        results[1] = x_in[BLOCKS - 1][1].bitcast(F32)
         turns = []
         x_ready, z_ready, multiplied = [], [], []
 
@@ -124,10 +127,10 @@ def tile_attend_gmw_kernel(tc, xT, dyT, hE, sw, tw, offs, offs2, out):
             return bank
 
         def turn_pairs(prod, rounded):
-            nc.scalar.copy(out=rounded[:].rearrange("p (u s e) -> p u s e", u=2, e=2),
+            nc.scalar.copy(out=rounded.rearrange("p (u s e) -> p u s e", u=2, e=2),
                            in_=prod.rearrange("p (s u e) -> p u s e", u=2, e=2))
             bank = next_bank().rearrange("p (t d) -> p t d", t=PACK)
-            words = rounded[:].bitcast(F32)
+            words = rounded.bitcast(F32)
             for u in range(2):
                 nc.tensor.transpose(bank[:, u, :], words[:, u * P:(u + 1) * P], ident[:])
             return bank
@@ -215,8 +218,8 @@ def tile_attend_gmw_kernel(tc, xT, dyT, hE, sw, tw, offs, offs2, out):
             x_gather(head[g], 0, g, 1)
             floats_out(0, g, turn_floats(head[g]))
             x_quantise(0, g, 1)
-        x_left = [(1, 0), (1, 1), (2, 0), (2, 1), (3, 0), (3, 1), (1, 2), (1, 3), (2, 2), (3, 2), (2, 3), (3, 3)]
-        counts = [0, 2, 2, 2, 2, 2, 0]
+        x_left = [(b, g) for b in range(1, BLOCKS) for g in range(PASSES - 1)] + [(b, PASSES - 1) for b in range(BLOCKS)]
+        counts = [0, 2, 2, 2, 2, 2, 1]
         late = None
 
         def finish_late(unit):
@@ -240,18 +243,18 @@ def tile_attend_gmw_kernel(tc, xT, dyT, hE, sw, tw, offs, offs2, out):
             now = None
             if len(units) == 2:
                 now = units[0] + (turn_floats(slab[:, 0:PASS]),)
-            if units:
-                late = units[-1] + (turn_pairs(slab[:, (len(units) - 1) * PASS:len(units) * PASS], pairs[r % 2]),)
-            if True and r + 2 == LAST:
+            if False and r + 2 == LAST:
                 relu(LAST)
             z_weave(r)
             g, j = Z_ORDER[r]
             if j == 1:
                 z_quantise(g)
+            if units:
+                late = units[-1] + (turn_pairs(slab[:, (len(units) - 1) * PASS:len(units) * PASS], pairs[r % 2]),)
             if now is not None:
                 floats_out(*now)
                 x_quantise(now[0], now[1], 1)
-            if r + 2 < ROUNDS and not (True and r + 2 == LAST):
+            if r + 2 < ROUNDS and not (False and r + 2 == LAST):
                 relu(r + 2)
         if late is not None:
             finish_late(late)
@@ -260,7 +263,7 @@ def tile_attend_gmw_kernel(tc, xT, dyT, hE, sw, tw, offs, offs2, out):
         units = x_left[-2:]
         for k, (b, g) in enumerate(units):
             x_gather(hs[LAST][:, k * PASS:(k + 1) * PASS], b, g, 1)
-        z_block_on_scalar(LAST, 0)
+        z_block_on_vector(LAST, 0)
         z_block_on_vector(LAST, 1)
         last = [turn_pairs(hs[LAST][:, k * PASS:(k + 1) * PASS], pairs[k]) for k in range(2)]
         z_quantise(PASSES - 1)
@@ -268,7 +271,7 @@ def tile_attend_gmw_kernel(tc, xT, dyT, hE, sw, tw, offs, offs2, out):
             finish_late(units[k] + (last[k],))
         for b in range(BLOCKS):
             if b % 2 == 1:
-                nc.vector.tensor_copy(out=results[b][:], in_=acc[b][:])
+                nc.vector.tensor_copy(out=results[b], in_=acc[b][:])
             else:
-                nc.scalar.copy(out=results[b][:], in_=acc[b][:])
-            nc.sync.dma_start(out=out[b * P:(b + 1) * P, :], in_=results[b][:])
+                nc.scalar.copy(out=results[b], in_=acc[b][:])
+            nc.sync.dma_start(out=out[b * P:(b + 1) * P, :], in_=results[b])

@@ -3,8 +3,9 @@ from contextlib import ExitStack
 import concourse.mybir as mybir
 from concourse.masks import make_identity
 
-V, E, D, DV = 1024, 2048, 512, 512
-FLOPS = 2 * E * D * DV
+NODES, EDGES, D, DV = 1024, 2048, 512, 512
+FLOPS = 2 * EDGES * D * DV
+BYTES = 4 * (D * NODES + DV * NODES + DV * EDGES + D * DV + 2 * EDGES) + 2 * 2 * 8 * EDGES
 
 F32 = mybir.dt.float32
 BF16 = mybir.dt.bfloat16
@@ -20,16 +21,24 @@ RELU = mybir.ActivationFunctionType.Relu
 P = 128
 PACK = 4
 PASS = P * PACK
-PASSES = E // PASS
+PASSES = EDGES // PASS
 BLOCKS = D // P
-COLS = PASS // 16
+LIST_COLS = PASS // 16
 ROUNDS = 2 * PASSES
 LAST = ROUNDS - 1
 BANKS = 4
-HEAD = 3
 SLABS = 3
+HEAD = 3
+TAIL = 2
 PAD = 32
-Z_ORDER = [(0, 0), (1, 0), (0, 1), (1, 1), (2, 0), (2, 1), (3, 0), (3, 1)]
+
+ROUND_WORK = [(0, 0), (1, 0), (0, 1), (1, 1)] + [(g, j) for g in range(2, PASSES) for j in range(2)]
+X_UNITS = [(b, g) for b in range(BLOCKS) for g in range(PASSES - 1)] + [(b, PASSES - 1) for b in range(BLOCKS)]
+
+
+def round_units(r):
+    first = HEAD + 2 * (r - 1)
+    return X_UNITS[first:min(first + 2, len(X_UNITS) - TAIL)] if r > 0 else []
 
 
 def tile_attend_gmw_kernel(tc, xT, dyT, hE, sw, tw, offs, offs2, out):
@@ -38,166 +47,148 @@ def tile_attend_gmw_kernel(tc, xT, dyT, hE, sw, tw, offs, offs2, out):
         held = ctx.enter_context(tc.tile_pool(name="held", bufs=1))
         psum = ctx.enter_context(tc.psum_pool(name="psum", bufs=1))
 
-        src = held.tile([P, E // 16], U16, name="src")
-        dst = held.tile([P, E // 16], U16, name="dst")
-        xw = [held.tile([P, V + PAD], F32, name="xw%d" % b) for b in range(BLOCKS)]
-        dyw = [held.tile([P, V], F32, name="dyw%d" % b) for b in range(BLOCKS)]
-        sws = held.tile([P, E], F32, name="sws")
-        hs = [held.tile([P, 2 * PASS], F32, name="h%d" % r, align_bytes=64) for r in range(ROUNDS)]
-        slabs = [held.tile([P, 2 * PASS], F32, name="slab%d" % k) for k in range(SLABS)]
-        twc = held.tile([P, PASSES * PACK], F32, name="twc")
+        src = held.tile([P, EDGES // 16], U16, name="src")
+        dst = held.tile([P, EDGES // 16], U16, name="dst")
+        x_tables = [held.tile([P, NODES + PAD], F32, name="x_table%d" % b) for b in range(BLOCKS)]
+        dy_tables = [held.tile([P, NODES], F32, name="dy_table%d" % b) for b in range(BLOCKS)]
+        sw_rows = held.tile([P, EDGES], F32, name="sw_rows")
+        h_raw = [held.tile([P, 2 * PASS], F32, name="h%d" % r, align_bytes=64) for r in range(ROUNDS)]
+        slab_row = held.tile([P, SLABS * 2 * PASS], F32, name="slab_row")
+        slabs = [slab_row[:, k * 2 * PASS:(k + 1) * 2 * PASS] for k in range(SLABS)]
+        head_home = held.tile([P, PASS], F32, name="head_home")
+        tw_cols = held.tile([P, PASSES * PACK], F32, name="twc")
+        sw_lines = held.tile([P, P], F32, name="sw_lines")
+        sw_cols = slab_row[:, 2 * PASS - 2 * PACK:2 * PASS + PACK]
         ident = held.tile([P, P], F32, name="ident")
+        for table in x_tables:
+            nc.gpsimd.memset(table[:, NODES:NODES + PAD], 0.0)
         make_identity(nc, ident[:])
-        for b in range(1, BLOCKS):
-            nc.gpsimd.memset(xw[b][:, V:V + PAD], 0.0)
-        nc.gpsimd.memset(xw[0][:, V:V + PAD], 0.0)
 
-        def load_sw(g):
-            nc.sync.dma_start(out=sws[:, g * PASS:(g + 1) * PASS], in_=sw[:, g * PASS:(g + 1) * PASS])
+        loaded = []
 
         def load_h(r):
-            g, j = Z_ORDER[r]
-            nc.sync.dma_start(out=hs[r][:].rearrange("p (i e) -> p i e", i=2),
+            g, j = ROUND_WORK[r]
+            nc.sync.dma_start(out=h_raw[r][:].rearrange("p (i e) -> p i e", i=2),
                               in_=hE[2 * j * P:2 * (j + 1) * P, g * PASS:(g + 1) * PASS].rearrange("(i p) e -> p i e", p=P))
 
-        def load_small():
-            nc.sync.dma_start(out=twc[:].rearrange("p (g t) -> p g t", t=PACK),
-                              in_=tw[0, :].rearrange("(g p t) -> p g t", p=P, t=PACK))
+        def load_table(tile, table, b):
+            if tile not in loaded:
+                loaded.append(tile)
+                nc.sync.dma_start(out=tile[:, 0:NODES], in_=table[b * P:(b + 1) * P, :])
 
-        def load_table(tiles, table, b):
-            nc.sync.dma_start(out=tiles[b][:, 0:V], in_=table[b * P:(b + 1) * P, :])
-
-        load_table(xw, xT, 0)
+        nc.sync.dma_start(out=sw_lines[:], in_=sw[0:P * P // EDGES, :].rearrange("a (r p) -> (a r) p", p=P))
+        load_table(x_tables[0], xT, 0)
         nc.sync.dma_start(src[:], offs)
-        load_sw(0)
-        load_sw(1)
+        nc.sync.dma_start(out=sw_rows[:, 0:PASS], in_=sw[:, 0:PASS])
         load_h(0)
-        load_sw(2)
-        load_h(1)
-        nc.sync.dma_start(dst[:], offs2)
-        load_table(dyw, dyT, 0)
-        load_table(dyw, dyT, 1)
-        load_small()
-        load_h(2)
-        load_table(xw, xT, 1)
-        load_table(dyw, dyT, 2)
-        load_table(dyw, dyT, 3)
-        load_table(xw, xT, 2)
-        load_h(3)
-        load_table(xw, xT, 3)
-        load_h(4)
-        load_sw(3)
-        load_h(5)
-        load_h(6)
-        load_h(7)
+        nc.sync.dma_start(out=tw_cols[:].rearrange("p (g t) -> p g t", t=PACK),
+                          in_=tw[0, :].rearrange("(g p t) -> p g t", p=P, t=PACK))
+        for r in range(LAST):
+            load_h(r + 1)
+            if r == 0:
+                nc.sync.dma_start(dst[:], offs2)
+            for i in range(2):
+                b = 2 * ROUND_WORK[r][1] + i
+                load_table(dy_tables[b], dyT, b)
+            for b, g in round_units(r):
+                load_table(x_tables[b], xT, b)
 
         x_words = [held.tile([P, PASSES * P], U32, name="xq%d" % b, align_bytes=64) for b in range(BLOCKS)]
         x_scales = [held.tile([P, PASSES * P], U8, name="xs%d" % b, align_bytes=64) for b in range(BLOCKS)]
-        x_in = [[held.tile([P, 2 * PASS], BF16, name="xi%d_%d" % (b, h), align_bytes=64)[:] for h in range(2)] for b in range(BLOCKS)]
-        x_in[0] = [hs[h][:, 0:PASS].bitcast(BF16) for h in range(2)]
-        spare = held.tile([P, 2 * PASS], F32, name="spare")
-        z_words = [held.tile([P, DV], U32, name="zq%d" % g, align_bytes=64)[:] for g in range(PASSES)]
+        x_in = [[h_raw[k][:, 0:PASS].bitcast(BF16) for k in range(2)]]
+        x_in.extend([held.tile([P, 2 * PASS], BF16, name="xi%d_%d" % (b, k), align_bytes=64)[:] for k in range(2)]
+                    for b in range(1, BLOCKS))
+        z_words = [held.tile([P, DV], U32, name="zq%d" % g, align_bytes=64) for g in range(PASSES)]
         z_scales = [held.tile([P, DV], U8, name="zs%d" % g, align_bytes=64) for g in range(PASSES)]
         z_in = [held.tile([P, DV * PACK], BF16, name="zi%d" % g, align_bytes=64) for g in range(PASSES)]
         acc = [psum.tile([P, DV], F32, name="acc%d" % b) for b in range(BLOCKS)]
         banks = [psum.tile([P, PASS], F32, name="bank%d" % k) for k in range(BANKS)]
-        z_prod = [held.tile([P, PASS], F32, name="prod%d" % i, align_bytes=64) for i in range(2)]
+        z_homes = [held.tile([P, PASS], F32, name="z_home%d" % i) for i in range(2)]
         pair_bufs = [held.tile([P, PASS], F32, name="pairs%d" % i) for i in range(2)]
         pairs = [buf[:].bitcast(BF16)[:, 0:PASS] for buf in pair_bufs]
-        results = [held.tile([P, DV], F32, name="result%d" % b)[:] for b in range(BLOCKS)]
-        results[0] = pair_bufs[1][:]
-        results[1] = x_in[BLOCKS - 1][1].bitcast(F32)
-        turns = []
-        x_ready, z_ready, multiplied = [], [], []
+        results = [pair_bufs[1][:], x_in[BLOCKS - 1][1].bitcast(F32), pair_bufs[0][:], z_homes[0][:]]
+        turns, x_ready, z_ready, multiplied = [], [], [], []
 
         def next_bank():
             turns.append(banks[len(turns) % BANKS])
             return turns[-1][:]
 
-        def gather(prod, window, lst, g, passes, factor):
-            nc.vector.tensor_tensor(prod, window[:].indirect(lst[:, g * COLS:(g + passes) * COLS]), factor, MULT)
+        def gather(home, table, offsets, g, passes, factor):
+            looked_up = table[:].indirect(offsets[:, g * LIST_COLS:(g + passes) * LIST_COLS])
+            nc.vector.tensor_tensor(home, looked_up, factor, MULT)
 
-        def x_gather(prod, b, g, passes):
-            gather(prod, xw[b], src, g, passes, sws[:, g * PASS:(g + passes) * PASS])
+        def x_gather(home, b, g, passes):
+            gather(home, x_tables[b], src, g, passes, sw_rows[:, g * PASS:(g + passes) * PASS])
 
-        def turn_floats(prod):
+        def turn_floats(home):
             bank = next_bank().rearrange("p (t d) -> p t d", t=PACK)
             for t in range(PACK):
-                nc.tensor.transpose(bank[:, t, :], prod[:, t:PASS:PACK], ident[:])
+                nc.tensor.transpose(bank[:, t, :], home[:, t:PASS:PACK], ident[:])
             return bank
 
-        def turn_pairs(prod, rounded):
+        def turn_pairs(home, rounded):
             nc.scalar.copy(out=rounded.rearrange("p (u s e) -> p u s e", u=2, e=2),
-                           in_=prod.rearrange("p (s u e) -> p u s e", u=2, e=2))
-            bank = next_bank().rearrange("p (t d) -> p t d", t=PACK)
+                           in_=home.rearrange("p (s u e) -> p u s e", u=2, e=2))
+            bank = next_bank()[:, 0:2 * P].rearrange("p (u d) -> p u d", u=2)
             words = rounded.bitcast(F32)
             for u in range(2):
                 nc.tensor.transpose(bank[:, u, :], words[:, u * P:(u + 1) * P], ident[:])
             return bank
 
-        def floats_out(b, g, bank):
-            nc.scalar.copy(out=x_in[b][g // 2][:, g % 2 * PASS:(g % 2 + 1) * PASS].rearrange("p (d t) -> p d t", t=PACK),
-                           in_=bank.rearrange("p t d -> p d t"))
+        def x_slot(b, g):
+            return x_in[b][g // 2][:, g % 2 * PASS:(g % 2 + 1) * PASS]
 
-        def pairs_out(b, g, bank):
-            nc.scalar.copy(out=x_in[b][g // 2][:, g % 2 * PASS:(g % 2 + 1) * PASS].bitcast(F32).rearrange("p (d u) -> p d u", u=2),
-                           in_=bank[:, 0:2, :].rearrange("p u d -> p d u"))
-
-        def x_quantise(b, g, passes):
-            cols = slice(g * P, (g + passes) * P)
-            nc.vector.quantize_mx(out=x_words[b][:, cols].bitcast(E4M3), scales=x_scales[b][:, cols],
-                                  in_=x_in[b][g // 2][:, g % 2 * PASS:(g % 2 + passes) * PASS])
-            x_ready.extend((b, g + k) for k in range(passes))
+        def x_quantise(b, g):
+            cols = slice(g * P, (g + 1) * P)
+            nc.vector.quantize_mx(out=x_words[b][:, cols].bitcast(E4M3), scales=x_scales[b][:, cols], in_=x_slot(b, g))
+            x_ready.append((b, g))
             multiply_ready()
 
+        def finish_floats(b, g, bank):
+            nc.scalar.copy(out=x_slot(b, g).rearrange("p (d t) -> p d t", t=PACK), in_=bank.rearrange("p t d -> p d t"))
+            x_quantise(b, g)
+
+        def finish_pairs(b, g, bank):
+            nc.scalar.copy(out=x_slot(b, g).bitcast(F32).rearrange("p (d u) -> p d u", u=2),
+                           in_=bank.rearrange("p u d -> p d u"))
+            x_quantise(b, g)
+
         def relu(r):
-            nc.scalar.activation(out=slabs[r % SLABS][:], in_=hs[r][:], func=RELU, scale=2.0)
+            nc.scalar.activation(out=slabs[r % SLABS], in_=h_raw[r][:], func=RELU, scale=2.0)
 
         def z_gather(r, i):
-            g, j = Z_ORDER[r]
-            gather(z_prod[i][:], dyw[2 * j + i], dst, g, 1, slabs[r % SLABS][:, i * PASS:(i + 1) * PASS])
-
-        def tw_column(g, t):
-            return twc[:, g * PACK + t:g * PACK + t + 1]
+            g, j = ROUND_WORK[r]
+            gather(z_homes[i][:], dy_tables[2 * j + i], dst, g, 1, slabs[r % SLABS][:, i * PASS:(i + 1) * PASS])
 
         def planes(r):
-            return slabs[r % SLABS][:].bitcast(BF16).rearrange("p (h t n) -> p h t n", h=2, n=2 * P)[:, :, 0:2, :]
+            return slabs[r % SLABS].bitcast(BF16).rearrange("p (h t n) -> p h t n", h=2, n=2 * P)[:, :, 0:2, :]
 
         def z_turn_and_scale(r):
-            g, j = Z_ORDER[r]
+            g = ROUND_WORK[r][0]
             two = [next_bank().rearrange("p (t n) -> p t n", t=2) for h in range(2)]
             for i in range(2):
                 for t in range(PACK):
-                    nc.tensor.transpose(two[t // 2][:, t % 2, i * P:(i + 1) * P], z_prod[i][:, t:PASS:PACK], ident[:])
+                    nc.tensor.transpose(two[t // 2][:, t % 2, i * P:(i + 1) * P], z_homes[i][:, t:PASS:PACK], ident[:])
             for t in range(PACK):
                 nc.scalar.activation(out=planes(r)[:, t // 2, t % 2, :], in_=two[t // 2][:, t % 2, :], func=COPY,
-                                     scale=tw_column(g, t))
+                                     scale=tw_cols[:, g * PACK + t:g * PACK + t + 1])
 
         def z_weave(r):
-            g, j = Z_ORDER[r]
-            nc.scalar.copy(out=z_in[g][:, j * 2 * PASS:(j + 1) * 2 * PASS].rearrange("p (c i h t) -> p c h t i", i=4, h=2, t=2),
+            g, j = ROUND_WORK[r]
+            woven = z_in[g][:, j * 2 * PASS:(j + 1) * 2 * PASS]
+            nc.scalar.copy(out=woven.rearrange("p (c i h t) -> p c h t i", i=4, h=2, t=2),
                            in_=planes(r).rearrange("p h t (c i) -> p c h t i", i=4))
 
-        def z_block_on_scalar(r, i):
-            g, j = Z_ORDER[r]
-            bank = turn_floats(z_prod[i][:])
-            flat = slabs[r % SLABS][:, i * PASS:(i + 1) * PASS].bitcast(BF16)[:, 0:PASS].rearrange("p (t n) -> p t n", t=PACK)
-            for t in range(PACK):
-                nc.scalar.activation(out=flat[:, t, :], in_=bank[:, t, :], func=COPY, scale=tw_column(g, t))
+        def z_unit_on_vector(r, i):
+            g, j = ROUND_WORK[r]
             b = 2 * j + i
-            nc.scalar.copy(out=z_in[g][:, b * PASS:(b + 1) * PASS].rearrange("p (c i t) -> p c t i", i=4, t=PACK),
-                           in_=flat.rearrange("p t (c i) -> p c t i", i=4))
-
-        def z_block_on_vector(r, i):
-            g, j = Z_ORDER[r]
-            b = 2 * j + i
-            bank = turn_floats(z_prod[i][:])
+            bank = turn_floats(z_homes[i][:])
             nc.vector.tensor_tensor(z_in[g][:, b * PASS:(b + 1) * PASS].rearrange("p (n t) -> p n t", t=PACK),
                                     bank.rearrange("p t n -> p n t"),
-                                    twc[:, g * PACK:(g + 1) * PACK].unsqueeze(1).to_broadcast([P, P, PACK]), MULT)
+                                    tw_cols[:, g * PACK:(g + 1) * PACK].unsqueeze(1).to_broadcast([P, P, PACK]), MULT)
 
         def z_quantise(g):
-            nc.vector.quantize_mx(out=z_words[g].bitcast(E5M2), scales=z_scales[g][:], in_=z_in[g][:])
+            nc.vector.quantize_mx(out=z_words[g][:].bitcast(E5M2), scales=z_scales[g][:], in_=z_in[g][:])
             z_ready.append(g)
             multiply_ready()
 
@@ -206,69 +197,67 @@ def tile_attend_gmw_kernel(tc, xT, dyT, hE, sw, tw, offs, offs2, out):
                 for b in range(BLOCKS):
                     if (b, g) in x_ready and (b, g) not in multiplied:
                         cols = slice(g * P, (g + 1) * P)
-                        nc.tensor.matmul_mx(out=acc[b][:], lhsT=x_words[b][:, cols].bitcast(E4M3), lhsT_scale=x_scales[b][:, cols],
-                                            rhs=z_words[g].bitcast(E5M2), rhs_scale=z_scales[g][:],
+                        nc.tensor.matmul_mx(out=acc[b][:],
+                                            lhsT=x_words[b][:, cols].bitcast(E4M3), lhsT_scale=x_scales[b][:, cols],
+                                            rhs=z_words[g][:].bitcast(E5M2), rhs_scale=z_scales[g][:],
                                             start=(g == 0), stop=(g == PASSES - 1))
                         multiplied.append((b, g))
 
+        bank = next_bank()
+        nc.tensor.transpose(bank[:, 0:P], sw_lines[:], ident[:])
+        nc.scalar.copy(out=sw_cols, in_=bank[:, PACK:EDGES // P])
+        for g in range(1, PASSES):
+            bank = next_bank()
+            for c in range(PACK):
+                column = sw_cols[:, (g - 1) * PACK + c:(g - 1) * PACK + c + 1]
+                nc.tensor.transpose(bank[:, c * P:(c + 1) * P], column.to_broadcast([P, P]), ident[:])
+            nc.scalar.copy(out=sw_rows[:, g * PASS:(g + 1) * PASS], in_=bank)
+
         relu(0)
         relu(1)
-        head = [z_prod[0][:], z_prod[1][:], slabs[2][:, 0:PASS], slabs[2][:, PASS:2 * PASS]]
-        for g in range(HEAD):
-            x_gather(head[g], 0, g, 1)
-            floats_out(0, g, turn_floats(head[g]))
-            x_quantise(0, g, 1)
-        x_left = [(b, g) for b in range(1, BLOCKS) for g in range(PASSES - 1)] + [(b, PASSES - 1) for b in range(BLOCKS)]
-        counts = [0, 2, 2, 2, 2, 2, 1]
+        homes = [slabs[2][:, 0:PASS], slabs[2][:, PASS:2 * PASS], head_home[:]]
+        for (b, g), home in zip(X_UNITS[:HEAD], homes):
+            x_gather(home, b, g, 1)
+            finish_floats(b, g, turn_floats(home))
+
         late = None
-
-        def finish_late(unit):
-            pairs_out(*unit)
-            x_quantise(unit[0], unit[1], 1)
-
         for r in range(LAST):
             z_gather(r, 0)
             z_gather(r, 1)
             z_turn_and_scale(r)
             if late is not None:
-                finish_late(late)
-                late = None
-            units = x_left[sum(counts[:r]):sum(counts[:r + 1])]
-            slab = slabs[(r - 1) % SLABS] if r > 1 else spare
-            if PAD and len(units) == 2 and units[1] == (units[0][0], units[0][1] + 1):
-                x_gather(slab[:], units[0][0], units[0][1], 2)
+                finish_pairs(*late)
+            units = round_units(r)
+            both = slabs[(r - 1) % SLABS] if r > 1 else h_raw[1][:]
+            homes = [both[:, k * PASS:(k + 1) * PASS] for k in range(len(units))]
+            if len(units) == 2 and units[0][0] == units[1][0]:
+                x_gather(both, units[0][0], units[0][1], 2)
             else:
-                for k, (b, g) in enumerate(units):
-                    x_gather(slab[:, k * PASS:(k + 1) * PASS], b, g, 1)
-            now = None
-            if len(units) == 2:
-                now = units[0] + (turn_floats(slab[:, 0:PASS]),)
-            if False and r + 2 == LAST:
-                relu(LAST)
+                for (b, g), home in zip(units, homes):
+                    x_gather(home, b, g, 1)
+            early = [unit + (turn_floats(home),) for unit, home in zip(units[:-1], homes)]
             z_weave(r)
-            g, j = Z_ORDER[r]
+            g, j = ROUND_WORK[r]
             if j == 1:
                 z_quantise(g)
-            if units:
-                late = units[-1] + (turn_pairs(slab[:, (len(units) - 1) * PASS:len(units) * PASS], pairs[r % 2]),)
-            if now is not None:
-                floats_out(*now)
-                x_quantise(now[0], now[1], 1)
-            if r + 2 < ROUNDS and not (False and r + 2 == LAST):
+            late = units[-1] + (turn_pairs(homes[-1], pairs[r % 2]),) if units else None
+            for unit in early:
+                finish_floats(*unit)
+            if r + 2 < ROUNDS:
                 relu(r + 2)
-        if late is not None:
-            finish_late(late)
+        finish_pairs(*late)
+
         z_gather(LAST, 0)
         z_gather(LAST, 1)
-        units = x_left[-2:]
-        for k, (b, g) in enumerate(units):
-            x_gather(hs[LAST][:, k * PASS:(k + 1) * PASS], b, g, 1)
-        z_block_on_vector(LAST, 0)
-        z_block_on_vector(LAST, 1)
-        last = [turn_pairs(hs[LAST][:, k * PASS:(k + 1) * PASS], pairs[k]) for k in range(2)]
+        homes = [h_raw[LAST][:, k * PASS:(k + 1) * PASS] for k in range(TAIL)]
+        for (b, g), home in zip(X_UNITS[-TAIL:], homes):
+            x_gather(home, b, g, 1)
+        z_unit_on_vector(LAST, 0)
+        z_unit_on_vector(LAST, 1)
+        turned = [turn_pairs(homes[k], pairs[k]) for k in range(TAIL)]
         z_quantise(PASSES - 1)
-        for k in range(2):
-            finish_late(units[k] + (last[k],))
+        for unit, bank in zip(X_UNITS[-TAIL:], turned):
+            finish_pairs(unit[0], unit[1], bank)
         for b in range(BLOCKS):
             if b % 2 == 1:
                 nc.vector.tensor_copy(out=results[b], in_=acc[b][:])

from contextlib import ExitStack

import concourse.mybir as mybir
from concourse.masks import make_identity

NODES, EDGES, D, DV = 1024, 2048, 512, 512
FLOPS = 2 * EDGES * D * DV
BYTES = 4 * (D * NODES + DV * NODES + DV * EDGES + D * DV + 2 * EDGES) + 2 * 2 * 8 * EDGES

F32 = mybir.dt.float32
BF16 = mybir.dt.bfloat16
U32 = mybir.dt.uint32
U16 = mybir.dt.uint16
U8 = mybir.dt.uint8
E4M3 = mybir.dt.float8_e4m3fn_x4
E5M2 = mybir.dt.float8_e5m2_x4
MULT = mybir.AluOpType.mult
COPY = mybir.ActivationFunctionType.Copy
RELU = mybir.ActivationFunctionType.Relu

P = 128
PACK = 4
PASS = P * PACK
PASSES = EDGES // PASS
BLOCKS = D // P
LIST_COLS = PASS // 16
ROUNDS = 2 * PASSES
LAST = ROUNDS - 1
BANKS = 4
SLABS = 3
HEAD = 3
TAIL = 2
PAD = 32

ROUND_WORK = [(0, 0), (1, 0), (0, 1), (1, 1)] + [(g, j) for g in range(2, PASSES) for j in range(2)]
X_UNITS = [(b, g) for b in range(BLOCKS) for g in range(PASSES - 1)] + [(b, PASSES - 1) for b in range(BLOCKS)]


def round_units(r):
    first = HEAD + 2 * (r - 1)
    return X_UNITS[first:min(first + 2, len(X_UNITS) - TAIL)] if r > 0 else []


def tile_attend_gmw_kernel(tc, xT, dyT, hE, sw, tw, offs, offs2, out):
    nc = tc.nc
    with ExitStack() as ctx:
        held = ctx.enter_context(tc.tile_pool(name="held", bufs=1))
        psum = ctx.enter_context(tc.psum_pool(name="psum", bufs=1))

        src = held.tile([P, EDGES // 16], U16, name="src")
        dst = held.tile([P, EDGES // 16], U16, name="dst")
        x_tables = [held.tile([P, NODES + PAD], F32, name="x_table%d" % b) for b in range(BLOCKS)]
        dy_tables = [held.tile([P, NODES], F32, name="dy_table%d" % b) for b in range(BLOCKS)]
        sw_rows = held.tile([P, EDGES], F32, name="sw_rows")
        h_raw = [held.tile([P, 2 * PASS], F32, name="h%d" % r, align_bytes=64) for r in range(ROUNDS)]
        slab_row = held.tile([P, SLABS * 2 * PASS], F32, name="slab_row")
        slabs = [slab_row[:, k * 2 * PASS:(k + 1) * 2 * PASS] for k in range(SLABS)]
        head_home = held.tile([P, PASS], F32, name="head_home")
        tw_cols = held.tile([P, PASSES * PACK], F32, name="twc")
        sw_lines = held.tile([P, P], F32, name="sw_lines")
        sw_cols = slab_row[:, 2 * PASS - 2 * PACK:2 * PASS + PACK]
        ident = held.tile([P, P], F32, name="ident")
        for table in x_tables:
            nc.gpsimd.memset(table[:, NODES:NODES + PAD], 0.0)
        make_identity(nc, ident[:])

        loaded = []

        def load_h(r):
            g, j = ROUND_WORK[r]
            nc.sync.dma_start(out=h_raw[r][:].rearrange("p (i e) -> p i e", i=2),
                              in_=hE[2 * j * P:2 * (j + 1) * P, g * PASS:(g + 1) * PASS].rearrange("(i p) e -> p i e", p=P))

        def load_table(tile, table, b):
            if tile not in loaded:
                loaded.append(tile)
                nc.sync.dma_start(out=tile[:, 0:NODES], in_=table[b * P:(b + 1) * P, :])

        nc.sync.dma_start(out=sw_lines[:], in_=sw[0:P * P // EDGES, :].rearrange("a (r p) -> (a r) p", p=P))
        load_table(x_tables[0], xT, 0)
        nc.sync.dma_start(src[:], offs)
        nc.sync.dma_start(out=sw_rows[:, 0:PASS], in_=sw[:, 0:PASS])
        load_h(0)
        nc.sync.dma_start(out=tw_cols[:].rearrange("p (g t) -> p g t", t=PACK),
                          in_=tw[0, :].rearrange("(g p t) -> p g t", p=P, t=PACK))
        for r in range(LAST):
            load_h(r + 1)
            if r == 0:
                nc.sync.dma_start(dst[:], offs2)
            for i in range(2):
                b = 2 * ROUND_WORK[r][1] + i
                load_table(dy_tables[b], dyT, b)
            for b, g in round_units(r):
                load_table(x_tables[b], xT, b)

        x_words = [held.tile([P, PASSES * P], U32, name="xq%d" % b, align_bytes=64) for b in range(BLOCKS)]
        x_scales = [held.tile([P, PASSES * P], U8, name="xs%d" % b, align_bytes=64) for b in range(BLOCKS)]
        x_in = [[h_raw[k][:, 0:PASS].bitcast(BF16) for k in range(2)]]
        x_in.extend([held.tile([P, 2 * PASS], BF16, name="xi%d_%d" % (b, k), align_bytes=64)[:] for k in range(2)]
                    for b in range(1, BLOCKS))
        z_words = [held.tile([P, DV], U32, name="zq%d" % g, align_bytes=64) for g in range(PASSES)]
        z_scales = [held.tile([P, DV], U8, name="zs%d" % g, align_bytes=64) for g in range(PASSES)]
        z_in = [held.tile([P, DV * PACK], BF16, name="zi%d" % g, align_bytes=64) for g in range(PASSES)]
        acc = [psum.tile([P, DV], F32, name="acc%d" % b) for b in range(BLOCKS)]
        banks = [psum.tile([P, PASS], F32, name="bank%d" % k) for k in range(BANKS)]
        z_homes = [held.tile([P, PASS], F32, name="z_home%d" % i) for i in range(2)]
        pair_bufs = [held.tile([P, PASS], F32, name="pairs%d" % i) for i in range(2)]
        pairs = [buf[:].bitcast(BF16)[:, 0:PASS] for buf in pair_bufs]
        results = [pair_bufs[1][:], x_in[BLOCKS - 1][1].bitcast(F32), pair_bufs[0][:], z_homes[0][:]]
        turns, x_ready, z_ready, multiplied = [], [], [], []

        def next_bank():
            turns.append(banks[len(turns) % BANKS])
            return turns[-1][:]

        def gather(home, table, offsets, g, passes, factor):
            looked_up = table[:].indirect(offsets[:, g * LIST_COLS:(g + passes) * LIST_COLS])
            nc.vector.tensor_tensor(home, looked_up, factor, MULT)

        def x_gather(home, b, g, passes):
            gather(home, x_tables[b], src, g, passes, sw_rows[:, g * PASS:(g + passes) * PASS])

        def turn_floats(home):
            bank = next_bank().rearrange("p (t d) -> p t d", t=PACK)
            for t in range(PACK):
                nc.tensor.transpose(bank[:, t, :], home[:, t:PASS:PACK], ident[:])
            return bank

        def turn_pairs(home, rounded):
            nc.scalar.copy(out=rounded.rearrange("p (u s e) -> p u s e", u=2, e=2),
                           in_=home.rearrange("p (s u e) -> p u s e", u=2, e=2))
            bank = next_bank()[:, 0:2 * P].rearrange("p (u d) -> p u d", u=2)
            words = rounded.bitcast(F32)
            for u in range(2):
                nc.tensor.transpose(bank[:, u, :], words[:, u * P:(u + 1) * P], ident[:])
            return bank

        def x_slot(b, g):
            return x_in[b][g // 2][:, g % 2 * PASS:(g % 2 + 1) * PASS]

        def x_quantise(b, g):
            cols = slice(g * P, (g + 1) * P)
            nc.vector.quantize_mx(out=x_words[b][:, cols].bitcast(E4M3), scales=x_scales[b][:, cols], in_=x_slot(b, g))
            x_ready.append((b, g))
            multiply_ready()

        def finish_floats(b, g, bank):
            nc.scalar.copy(out=x_slot(b, g).rearrange("p (d t) -> p d t", t=PACK), in_=bank.rearrange("p t d -> p d t"))
            x_quantise(b, g)

        def finish_pairs(b, g, bank):
            nc.scalar.copy(out=x_slot(b, g).bitcast(F32).rearrange("p (d u) -> p d u", u=2),
                           in_=bank.rearrange("p u d -> p d u"))
            x_quantise(b, g)

        def relu(r):
            nc.scalar.activation(out=slabs[r % SLABS], in_=h_raw[r][:], func=RELU, scale=2.0)

        def z_gather(r, i):
            g, j = ROUND_WORK[r]
            gather(z_homes[i][:], dy_tables[2 * j + i], dst, g, 1, slabs[r % SLABS][:, i * PASS:(i + 1) * PASS])

        def planes(r):
            return slabs[r % SLABS].bitcast(BF16).rearrange("p (h t n) -> p h t n", h=2, n=2 * P)[:, :, 0:2, :]

        def z_turn_and_scale(r):
            g = ROUND_WORK[r][0]
            two = [next_bank().rearrange("p (t n) -> p t n", t=2) for h in range(2)]
            for i in range(2):
                for t in range(PACK):
                    nc.tensor.transpose(two[t // 2][:, t % 2, i * P:(i + 1) * P], z_homes[i][:, t:PASS:PACK], ident[:])
            for t in range(PACK):
                nc.scalar.activation(out=planes(r)[:, t // 2, t % 2, :], in_=two[t // 2][:, t % 2, :], func=COPY,
                                     scale=tw_cols[:, g * PACK + t:g * PACK + t + 1])

        def z_weave(r):
            g, j = ROUND_WORK[r]
            woven = z_in[g][:, j * 2 * PASS:(j + 1) * 2 * PASS]
            nc.scalar.copy(out=woven.rearrange("p (c i h t) -> p c h t i", i=4, h=2, t=2),
                           in_=planes(r).rearrange("p h t (c i) -> p c h t i", i=4))

        def z_unit_on_vector(r, i):
            g, j = ROUND_WORK[r]
            b = 2 * j + i
            bank = turn_floats(z_homes[i][:])
            nc.vector.tensor_tensor(z_in[g][:, b * PASS:(b + 1) * PASS].rearrange("p (n t) -> p n t", t=PACK),
                                    bank.rearrange("p t n -> p n t"),
                                    tw_cols[:, g * PACK:(g + 1) * PACK].unsqueeze(1).to_broadcast([P, P, PACK]), MULT)

        def z_quantise(g):
            nc.vector.quantize_mx(out=z_words[g][:].bitcast(E5M2), scales=z_scales[g][:], in_=z_in[g][:])
            z_ready.append(g)
            multiply_ready()

        def multiply_ready():
            for g in z_ready:
                for b in range(BLOCKS):
                    if (b, g) in x_ready and (b, g) not in multiplied:
                        cols = slice(g * P, (g + 1) * P)
                        nc.tensor.matmul_mx(out=acc[b][:],
                                            lhsT=x_words[b][:, cols].bitcast(E4M3), lhsT_scale=x_scales[b][:, cols],
                                            rhs=z_words[g][:].bitcast(E5M2), rhs_scale=z_scales[g][:],
                                            start=(g == 0), stop=(g == PASSES - 1))
                        multiplied.append((b, g))

        bank = next_bank()
        nc.tensor.transpose(bank[:, 0:P], sw_lines[:], ident[:])
        nc.scalar.copy(out=sw_cols, in_=bank[:, PACK:EDGES // P])
        for g in range(1, PASSES):
            bank = next_bank()
            for c in range(PACK):
                column = sw_cols[:, (g - 1) * PACK + c:(g - 1) * PACK + c + 1]
                nc.tensor.transpose(bank[:, c * P:(c + 1) * P], column.to_broadcast([P, P]), ident[:])
            nc.scalar.copy(out=sw_rows[:, g * PASS:(g + 1) * PASS], in_=bank)

        relu(0)
        relu(1)
        homes = [slabs[2][:, 0:PASS], slabs[2][:, PASS:2 * PASS], head_home[:]]
        for (b, g), home in zip(X_UNITS[:HEAD], homes):
            x_gather(home, b, g, 1)
            finish_floats(b, g, turn_floats(home))

        late = None
        for r in range(LAST):
            z_gather(r, 0)
            z_gather(r, 1)
            z_turn_and_scale(r)
            if late is not None:
                finish_pairs(*late)
            units = round_units(r)
            both = slabs[(r - 1) % SLABS] if r > 1 else h_raw[1][:]
            homes = [both[:, k * PASS:(k + 1) * PASS] for k in range(len(units))]
            if len(units) == 2 and units[0][0] == units[1][0]:
                x_gather(both, units[0][0], units[0][1], 2)
            else:
                for (b, g), home in zip(units, homes):
                    x_gather(home, b, g, 1)
            early = [unit + (turn_floats(home),) for unit, home in zip(units[:-1], homes)]
            z_weave(r)
            g, j = ROUND_WORK[r]
            if j == 1:
                z_quantise(g)
            late = units[-1] + (turn_pairs(homes[-1], pairs[r % 2]),) if units else None
            for unit in early:
                finish_floats(*unit)
            if r + 2 < ROUNDS:
                relu(r + 2)
        finish_pairs(*late)

        z_gather(LAST, 0)
        z_gather(LAST, 1)
        homes = [h_raw[LAST][:, k * PASS:(k + 1) * PASS] for k in range(TAIL)]
        for (b, g), home in zip(X_UNITS[-TAIL:], homes):
            x_gather(home, b, g, 1)
        z_unit_on_vector(LAST, 0)
        z_unit_on_vector(LAST, 1)
        turned = [turn_pairs(homes[k], pairs[k]) for k in range(TAIL)]
        z_quantise(PASSES - 1)
        for unit, bank in zip(X_UNITS[-TAIL:], turned):
            finish_pairs(unit[0], unit[1], bank)
        for b in range(BLOCKS):
            if b % 2 == 1:
                nc.vector.tensor_copy(out=results[b], in_=acc[b][:])
            else:
                nc.scalar.copy(out=results[b], in_=acc[b][:])
            nc.sync.dma_start(out=out[b * P:(b + 1) * P, :], in_=results[b])
